import numpy as np
import ml_dtypes


def mxq(x, axis, fmt="e4m3"):
    dtype, down = {"e4m3": (ml_dtypes.float8_e4m3fn, 7), "e5m2": (ml_dtypes.float8_e5m2, 14)}[fmt]
    v = np.moveaxis(np.asarray(x, np.float32).astype(ml_dtypes.bfloat16).astype(np.float64), axis, -1)
    blocks = v.reshape(v.shape[:-1] + (-1, 32))
    amax = np.abs(blocks).max(-1, keepdims=True)
    byte = np.maximum(np.where(amax > 0, np.frexp(amax)[1] - 1 + 127, 0) - down, 1)
    scale = np.exp2(byte - 127.0)
    codes = (blocks / scale).astype(np.float32).astype(dtype).astype(np.float64)
    return np.moveaxis((codes * scale).reshape(v.shape), -1, axis)


WIDE = False


def mx_kscale(k):
    if not WIDE:
        return np.ones(k)
    levels = np.array([10, -10, 5, -5, 0])
    if k % 512:
        return np.exp2(np.random.permutation(np.resize(levels, k // 32))).repeat(32)
    a = np.empty((k // 512, 16))
    for p in range(k // 512):
        a[p, :8] = np.random.permutation(np.resize(levels, 8))
        for g in range(8):
            far = levels[np.abs(levels - a[p, g]) >= 10]
            a[p, g + 8] = far[np.random.randint(len(far))]
    return np.exp2(a.ravel()).repeat(32)


def f64(x):
    return np.asarray(x).astype(np.float64)


def striped(idx):
    return np.tile(np.asarray(idx).reshape(-1, 16).T, (8, 1)).astype(np.uint16)


def unstriped(offs):
    return offs[:16].T.reshape(-1).astype(np.int64)


E2M1 = np.array([0.0, 0.5, 1.0, 1.5, 2.0, 3.0, 4.0, 6.0, -0.0, -0.5, -1.0, -1.5, -2.0, -3.0, -4.0, -6.0])


def pack_weight(w, fmt):
    k, n = w.shape
    w = f64(np.asarray(w, np.float32).astype(ml_dtypes.bfloat16)).reshape(k // 32, 32, n)
    amax = np.abs(w).max(1)
    if fmt == "e4m3":
        byte = np.frexp(amax)[1] - 1 + 127 - 7
    else:
        mant, ex = np.frexp(amax / 6.0)
        byte = np.where(mant > 0.5, ex, ex - 1) + 127
    byte = np.clip(np.where(amax > 0, byte, 1), 1, 254)
    scaled = (w * np.exp2(127.0 - byte)[:, None, :]).reshape(k, n).astype(np.float32)
    by_word = np.ascontiguousarray(scaled.reshape(k // 512, 128, 4, n).transpose(0, 1, 3, 2))
    if fmt == "e4m3":
        words = by_word.astype(ml_dtypes.float8_e4m3fn).view(np.uint8)
    else:
        c = by_word.astype(ml_dtypes.float4_e2m1fn).view(np.uint8) & 0xF
        words = (c[..., 0::2] | (c[..., 1::2] << 4)).reshape(k // 512, 128, 2 * n)
    return np.ascontiguousarray(words), np.ascontiguousarray(byte.astype(np.uint8).reshape(k // 512, 16, n))


def unpack_weight(words, scales, fmt):
    g, _, n = scales.shape
    words = np.ascontiguousarray(words).reshape(g, 128, n, -1)
    if fmt == "e4m3":
        vals = words.view(ml_dtypes.float8_e4m3fn).astype(np.float64)
    else:
        nib = np.empty((g, 128, n, 4), np.uint8)
        nib[..., 0::2] = words & 0xF
        nib[..., 1::2] = words >> 4
        vals = E2M1[nib]
    vals = vals * np.repeat(np.exp2(scales.astype(np.float64) - 127.0), 8, axis=1)[..., None]
    return vals.transpose(0, 1, 3, 2).reshape(g * 512, n)


def sigmoid(v):
    return 1.0 / (1.0 + np.exp(-v))


def bf(x):
    return np.asarray(x, np.float32).astype(ml_dtypes.bfloat16)


def planes(Y):
    r, m = Y.shape
    b = f64(bf(Y)).reshape(r // 32, 32, m)
    amax = np.abs(b).max(1)
    byte = np.clip(np.where(amax > 0, np.frexp(amax)[1] - 1 + 127 - 7, 1), 1, 254)
    codes = (b * np.exp2(127.0 - byte)[:, None, :]).reshape(r, m).astype(np.float32).astype(ml_dtypes.float8_e4m3fn).view(np.uint8)
    words = codes.reshape(r // 512, 128, 4, m).transpose(0, 1, 3, 2)
    return np.ascontiguousarray(words), np.ascontiguousarray(byte.astype(np.uint8).reshape(r // 512, 16, m))


K, T, J, L, N = 1024, 1024, 512, 512, 512


def setup_inputs():
    n = np.random.standard_normal
    idx = np.random.permutation(T)[:J]
    fk = mx_kscale(K)
    fl = mx_kscale(L)
    xqp = pack_weight(n((K, T)) / fk[:, None], "e2m1")
    xep = pack_weight(n((L, J)) / fl[:, None], "e4m3")
    wap = pack_weight(n((L, N)) * 1 / np.sqrt(L) * fl[:, None], "e2m1")
    return {
        "xq_words": xqp[0],
        "xq_scales": xqp[1],
        "ws": (n((K, N)) * 1 / np.sqrt(K) * fk[:, None]).astype(np.float32),
        "xe_words": xep[0],
        "xe_scales": xep[1],
        "wa_words": wap[0],
        "wa_scales": wap[1],
        "offs": striped(idx),
    }


def reference(xq_words, xq_scales, ws, xe_words, xe_scales, wa_words, wa_scales, offs):
    idx = unstriped(offs)
    xqu = unpack_weight(xq_words, xq_scales, "e2m1")
    xeu = unpack_weight(xe_words, xe_scales, "e4m3")
    wau = unpack_weight(wa_words, wa_scales, "e2m1")
    wsq = mxq(f64(ws), 0, "e4m3")
    u = wsq.T @ xqu
    p = wau.T @ xeu
    y = p * sigmoid(u[:, idx])
    words, scales = planes(y)
    return y, words, scales

@@ -1,0 +1,203 @@
+from contextlib import ExitStack
+
+import concourse.mybir as mybir
+
+K, T, J, L, N = 1024, 1024, 512, 512, 512
+FLOPS = 2 * K * N * T + 2 * L * N * J
+
+F32 = mybir.dt.float32
+BF16 = mybir.dt.bfloat16
+I32 = mybir.dt.int32
+U32 = mybir.dt.uint32
+U16 = mybir.dt.uint16
+U8 = mybir.dt.uint8
+FP8X4 = mybir.dt.float8_e4m3fn_x4
+FP4X4 = mybir.dt.float4_e2m1fn_x4
+SIGMOID = mybir.ActivationFunctionType.Sigmoid
+MULT = mybir.AluOpType.mult
+
+P = 128
+PACK = 4
+PASSES = K // (P * PACK)
+BANK = 512
+HALVES = T // BANK
+
+
+def tile_list_expert_under_shared_gate_pl_kernel(
+    tc, xq_words, xq_scales, ws, xe_words, xe_scales, wa_words, wa_scales, offs, out_0, out_1, out_2
+):
+    nc = tc.nc
+    with ExitStack() as ctx:
+        keep = ctx.enter_context(tc.tile_pool(name="keep", bufs=1))
+        psum = ctx.enter_context(tc.psum_pool(name="psum", bufs=1))
+
+        offsets = keep.tile([P, J // 16], U16, name="offsets")
+
+        row_runs = [[(0, 4)], [(0, 2), (2, 4)]]
+        ws_raw = [
+            [keep.tile([P, j1 - j0, N], F32, name="ws_raw%d%d" % (a, j0), align_bytes=64) for j0, j1 in row_runs[a]]
+            for a in range(PASSES)
+        ]
+        xq_sb = [keep.tile([P, 2 * T], U8, name="xq_sb%d" % a, align_bytes=64) for a in range(PASSES)]
+        xq_sc = keep.tile([P, PASSES, T], U8, name="xq_sc", align_bytes=64)
+        wa_raw = keep.tile([P, 2 * N], U8, name="wa_raw", align_bytes=64)
+        wa_sc_raw = keep.tile([P, N], U8, name="wa_sc_raw", align_bytes=64)
+        xe_sb = keep.tile([P, PACK * J], U8, name="xe_sb", align_bytes=64)
+        xe_sc = keep.tile([P, J], U8, name="xe_sc", align_bytes=64)
+
+        warm = keep.tile([P, 8], F32, name="warm")
+        warm_out = keep.tile([P, 8], F32, name="warm_out")
+        nc.vector.memset(warm[:], 0.0)
+        nc.vector.memset(wa_sc_raw[:].bitcast(U32), 0)
+
+        nc.sync.dma_start(offsets[:], offs)
+        nc.sync.dma_start(out=wa_raw[:].bitcast(I32), in_=wa_words[0].bitcast(I32))
+        for Q in range(4):
+            nc.scalar.dma_start(
+                out=xq_sc[32 * Q : 32 * Q + 4, :, :].bitcast(I32),
+                in_=xq_scales[:, 4 * Q : 4 * Q + 4, :].rearrange("z q c -> q z c").bitcast(I32),
+            )
+        for a in range(PASSES):
+            rows = ws[512 * a : 512 * (a + 1), :].rearrange("(p j) n -> p j n", j=PACK)
+            for raw, (j0, j1) in zip(ws_raw[a], row_runs[a]):
+                nc.sync.dma_start(out=raw[:], in_=rows[:, j0:j1, :])
+            nc.sync.dma_start(out=xq_sb[a][:].bitcast(I32), in_=xq_words[a].bitcast(I32))
+        nc.scalar.activation(warm_out[:], warm[:], SIGMOID)
+        nc.sync.dma_start(
+            out=xe_sb[:].bitcast(I32), in_=xe_words[0].rearrange("p c r -> p (c r)").bitcast(I32)
+        )
+        for Q in range(4):
+            nc.sync.dma_start(
+                out=wa_sc_raw[32 * Q : 32 * Q + 4, :].bitcast(I32),
+                in_=wa_scales[0, 4 * Q : 4 * Q + 4, :].bitcast(I32),
+            )
+        for Q in range(4):
+            nc.sync.dma_start(
+                out=xe_sc[32 * Q : 32 * Q + 4, :].bitcast(I32),
+                in_=xe_scales[0, 4 * Q : 4 * Q + 4, :].bitcast(I32),
+            )
+
+        wa_sb = keep.tile([P, PACK, 2 * P], U8, name="wa_sb", align_bytes=64)
+        nc.vector.tensor_copy(
+            out=wa_sb[:].rearrange("p t (m b) -> p t m b", b=2),
+            in_=wa_raw[:].rearrange("p (m t b) -> p t m b", t=PACK, b=2),
+        )
+
+        u_bank = [
+            [psum.tile([P, BANK], F32, name="u_bank%d%d" % (t, h), tag="bank%d%d" % (t, h)) for h in range(HALVES)]
+            for t in range(PACK)
+        ]
+
+        for a in range(PASSES):
+            grouped = [
+                keep.tile([P, 2, P, PACK], BF16, name="ws_bf%d%d" % (a, u), tag="ws_bf%d%d" % (a, u), align_bytes=64) for u in range(2)
+            ]
+            for raw, (j0, j1) in zip(ws_raw[a], row_runs[a]):
+                src = raw[:].rearrange("p j (m t) -> p m j t", t=PACK)
+                dst = [g[:].rearrange("p t m j -> p m j t")[:, :, j0:j1, :] for g in grouped]
+                nc.vector.tensor_copy(out=dst[0], in_=src[:, :, :, 0:2])
+                nc.scalar.copy(out=dst[1], in_=src[:, :, :, 2:4])
+            codes = [keep.tile([P, 2 * P], U32, name="ws_codes%d%d" % (a, u), align_bytes=64) for u in range(2)]
+            scales = [keep.tile([P, 2 * P], U8, name="ws_scales%d%d" % (a, u), align_bytes=64) for u in range(2)]
+            for e in range(2):
+                nc.vector.quantize_mx(
+                    out=codes[0][:, P * e : P * (e + 1)].bitcast(FP8X4),
+                    scales=scales[0][:, P * e : P * (e + 1)],
+                    in_=grouped[0][:, e, :, :].rearrange("p m j -> p (m j)"),
+                )
+            nc.vector.quantize_mx(
+                out=codes[1][:].bitcast(FP8X4),
+                scales=scales[1][:],
+                in_=grouped[1][:].rearrange("p t m j -> p (t m j)"),
+            )
+            for t in range(PACK):
+                cols = slice(P * (t % 2), P * (t % 2 + 1))
+                for h in range(HALVES):
+                    nc.tensor.matmul_mx(
+                        out=u_bank[t][h][:],
+                        lhsT=codes[t // 2][:, cols].bitcast(FP8X4),
+                        lhsT_scale=scales[t // 2][:, cols],
+                        rhs=xq_sb[a][:, 2 * BANK * h : 2 * BANK * (h + 1)].bitcast(FP4X4),
+                        rhs_scale=xq_sc[:, a, BANK * h : BANK * (h + 1)],
+                        start=(a == 0),
+                        stop=(a == PASSES - 1),
+                    )
+
+        wa_sc = keep.tile([P, PACK, P], U8, name="wa_sc", tag="ws_bf11", align_bytes=64)
+        nc.gpsimd.tensor_copy(out=wa_sc[:], in_=wa_sc_raw[:].rearrange("p (m t) -> p t m", t=PACK))
+
+        u_sb = [keep.tile([P, T], F32, name="u_sb%d" % t, align_bytes=64) for t in range(PACK)]
+        gate = [keep.tile([P, J], F32, name="gate%d" % t, align_bytes=64) for t in range(PACK)]
+        y = keep.tile([P, PACK, J], F32, name="y", align_bytes=64)
+        y_bf = [keep.tile([P, J // 2, PACK], BF16, name="y_bf%d" % g, align_bytes=64) for g in range(2)]
+        y_codes = keep.tile([P, J], U32, name="y_codes", align_bytes=64)
+        y_scales = keep.tile([P, J], U8, name="y_scales", align_bytes=64)
+        out_rows = out_0.rearrange("(p t) j -> p t j", t=PACK)
+        out_words = out_1[0].rearrange("p c r -> p (c r)").bitcast(I32)
+        p_bank = []
+
+        def drain_u(t):
+            for h in range(HALVES):
+                cols = slice(BANK * h, BANK * (h + 1))
+                if h == 0 and t == 0:
+                    nc.scalar.copy(out=u_sb[t][:, cols], in_=u_bank[t][h][:])
+                else:
+                    nc.vector.tensor_copy(out=u_sb[t][:, cols], in_=u_bank[t][h][:])
+            bank = psum.tile([P, BANK], F32, name="p_bank%d" % t, tag="bank%d0" % t)
+            nc.tensor.matmul_mx(
+                out=bank[:],
+                lhsT=wa_sb[:, t, :].bitcast(FP4X4),
+                lhsT_scale=wa_sc[:, t, :],
+                rhs=xe_sb[:].bitcast(FP8X4),
+                rhs_scale=xe_sc[:],
+                start=True,
+                stop=True,
+            )
+            p_bank.append(bank)
+
+        def look_up(t, j0, j1):
+            nc.scalar.activation(gate[t][:, j0:j1], u_sb[t][:].indirect(offsets[:, j0 // 16 : j1 // 16]), SIGMOID)
+
+        def gated(t, j0, j1):
+            nc.vector.tensor_tensor(y[:, t, j0:j1], p_bank[t][:, j0:j1], gate[t][:, j0:j1], MULT)
+
+        def regroup(copy, j0, j1):
+            g, first = divmod(j0, J // 2)
+            copy(
+                out=y_bf[g][:, first : first + j1 - j0, :].rearrange("p (c i) t -> p c t i", i=4),
+                in_=y[:, :, j0:j1].rearrange("p t (c i) -> p c t i", i=4),
+            )
+
+        def planes(g):
+            cols = slice(g * J // 2, (g + 1) * J // 2)
+            nc.vector.quantize_mx(
+                out=y_codes[:, cols].bitcast(FP8X4),
+                scales=y_scales[:, cols],
+                in_=y_bf[g][:].rearrange("p c t -> p (c t)"),
+            )
+            nc.sync.dma_start(out=out_words[:, cols], in_=y_codes[:, cols].bitcast(I32))
+
+        for t in range(PACK):
+            drain_u(t)
+            if t < PACK - 1:
+                look_up(t, 0, J)
+        for t in range(PACK - 1):
+            gated(t, 0, J)
+            nc.sync.dma_start(out=out_rows[:, t, :], in_=y[:, t, :])
+        look_up(3, 0, J // 2)
+        look_up(3, J // 2, J)
+        gated(3, 0, J // 2)
+        regroup(nc.vector.tensor_copy, 0, 128)
+        regroup(nc.scalar.copy, 128, 256)
+        gated(3, J // 2, J)
+        nc.sync.dma_start(out=out_rows[:, 3, :], in_=y[:, 3, :])
+        regroup(nc.vector.tensor_copy, 256, 448)
+        regroup(nc.scalar.copy, 448, 512)
+        planes(0)
+        planes(1)
+        for Q in range(4):
+            queue = nc.sync if Q % 2 == 0 else nc.scalar
+            queue.dma_start(
+                out=out_2[0, 4 * Q : 4 * Q + 4, :].bitcast(I32),
+                in_=y_scales[32 * Q : 32 * Q + 4, :].bitcast(I32),
+            )

@@ -38,7 +38,12 @@ def tile_list_expert_under_shared_gate_pl_kernel(
             [keep.tile([P, j1 - j0, N], F32, name="ws_raw%d%d" % (a, j0), align_bytes=64) for j0, j1 in row_runs[a]]
             for a in range(PASSES)
         ]
-        xq_sb = [keep.tile([P, 2 * T], U8, name="xq_sb%d" % a, align_bytes=64) for a in range(PASSES)]
+        xq_first = [keep.tile([P, 2 * BANK], U8, name="xq_first%d" % h, align_bytes=64) for h in range(HALVES)]
+        xq_second = keep.tile([P, 2 * T], U8, name="xq_second", align_bytes=64)
+        xq_sb = [
+            [xq_first[h][:] for h in range(HALVES)],
+            [xq_second[:, 2 * BANK * h : 2 * BANK * (h + 1)] for h in range(HALVES)],
+        ]
         xq_sc = keep.tile([P, PASSES, T], U8, name="xq_sc", align_bytes=64)
         wa_raw = keep.tile([P, 2 * N], U8, name="wa_raw", align_bytes=64)
         wa_sc_raw = keep.tile([P, N], U8, name="wa_sc_raw", align_bytes=64)
@@ -51,43 +56,42 @@ def tile_list_expert_under_shared_gate_pl_kernel(
         nc.vector.memset(wa_sc_raw[:].bitcast(U32), 0)
 
         nc.sync.dma_start(offsets[:], offs)
-        nc.sync.dma_start(out=wa_raw[:].bitcast(I32), in_=wa_words[0].bitcast(I32))
-        for Q in range(4):
+        for r in range(4):
             nc.scalar.dma_start(
-                out=xq_sc[32 * Q : 32 * Q + 4, :, :].bitcast(I32),
-                in_=xq_scales[:, 4 * Q : 4 * Q + 4, :].rearrange("z q c -> q z c").bitcast(I32),
+                out=xq_sc[r:P:32, :, :].bitcast(I32),
+                in_=xq_scales[:, r:16:4, :].rearrange("z q c -> q z c").bitcast(I32),
             )
         for a in range(PASSES):
             rows = ws[512 * a : 512 * (a + 1), :].rearrange("(p j) n -> p j n", j=PACK)
             for raw, (j0, j1) in zip(ws_raw[a], row_runs[a]):
                 nc.sync.dma_start(out=raw[:], in_=rows[:, j0:j1, :])
-            nc.sync.dma_start(out=xq_sb[a][:].bitcast(I32), in_=xq_words[a].bitcast(I32))
+            nc.sync.dma_start(
+                out=xq_first[a][:].bitcast(I32), in_=xq_words[0, :, 2 * BANK * a : 2 * BANK * (a + 1)].bitcast(I32)
+            )
+            if a == 0:
+                nc.sync.dma_start(out=wa_raw[:].bitcast(I32), in_=wa_words[0].bitcast(I32))
+        nc.sync.dma_start(out=xq_second[:].bitcast(I32), in_=xq_words[1].bitcast(I32))
         nc.scalar.activation(warm_out[:], warm[:], SIGMOID)
         nc.sync.dma_start(
             out=xe_sb[:].bitcast(I32), in_=xe_words[0].rearrange("p c r -> p (c r)").bitcast(I32)
         )
-        for Q in range(4):
+        for r in range(4):
             nc.sync.dma_start(
-                out=wa_sc_raw[32 * Q : 32 * Q + 4, :].bitcast(I32),
-                in_=wa_scales[0, 4 * Q : 4 * Q + 4, :].bitcast(I32),
+                out=wa_sc_raw[r:P:32, :].bitcast(I32),
+                in_=wa_scales[0, r:16:4, :].bitcast(I32),
             )
-        for Q in range(4):
+        for r in range(4):
             nc.sync.dma_start(
-                out=xe_sc[32 * Q : 32 * Q + 4, :].bitcast(I32),
-                in_=xe_scales[0, 4 * Q : 4 * Q + 4, :].bitcast(I32),
+                out=xe_sc[r:P:32, :].bitcast(I32),
+                in_=xe_scales[0, r:16:4, :].bitcast(I32),
             )
-
-        wa_sb = keep.tile([P, PACK, 2 * P], U8, name="wa_sb", align_bytes=64)
-        nc.vector.tensor_copy(
-            out=wa_sb[:].rearrange("p t (m b) -> p t m b", b=2),
-            in_=wa_raw[:].rearrange("p (m t b) -> p t m b", t=PACK, b=2),
-        )
 
         u_bank = [
             [psum.tile([P, BANK], F32, name="u_bank%d%d" % (t, h), tag="bank%d%d" % (t, h)) for h in range(HALVES)]
             for t in range(PACK)
         ]
 
+        ws_codes, ws_scales = [], []
         for a in range(PASSES):
             grouped = [
                 keep.tile([P, 2, P, PACK], BF16, name="ws_bf%d%d" % (a, u), tag="ws_bf%d%d" % (a, u), align_bytes=64) for u in range(2)
@@ -110,17 +114,28 @@ def tile_list_expert_under_shared_gate_pl_kernel(
                 scales=scales[1][:],
                 in_=grouped[1][:].rearrange("p t m j -> p (t m j)"),
             )
-            for t in range(PACK):
-                cols = slice(P * (t % 2), P * (t % 2 + 1))
-                for h in range(HALVES):
+            ws_codes.append(codes)
+            ws_scales.append(scales)
+            if a == 0:
+                wa_sb = keep.tile([P, PACK, 2 * P], U8, name="wa_sb", tag="ws_bf01", align_bytes=64)
+                nc.vector.tensor_copy(
+                    out=wa_sb[:].rearrange("p t (m b) -> p t m b", b=2),
+                    in_=wa_raw[:].rearrange("p (m t b) -> p t m b", t=PACK, b=2),
+                )
+
+        for t in range(PACK):
+            cols = slice(P * (t % 2), P * (t % 2 + 1))
+            for h in range(HALVES):
+                order = [0, 1] if h == 0 or t == 0 else [1, 0]
+                for a in order:
                     nc.tensor.matmul_mx(
                         out=u_bank[t][h][:],
-                        lhsT=codes[t // 2][:, cols].bitcast(FP8X4),
-                        lhsT_scale=scales[t // 2][:, cols],
-                        rhs=xq_sb[a][:, 2 * BANK * h : 2 * BANK * (h + 1)].bitcast(FP4X4),
+                        lhsT=ws_codes[a][t // 2][:, cols].bitcast(FP8X4),
+                        lhsT_scale=ws_scales[a][t // 2][:, cols],
+                        rhs=xq_sb[a][h].bitcast(FP4X4),
                         rhs_scale=xq_sc[:, a, BANK * h : BANK * (h + 1)],
-                        start=(a == 0),
-                        stop=(a == PASSES - 1),
+                        start=(a == order[0]),
+                        stop=(a == order[-1]),
                     )
 
         wa_sc = keep.tile([P, PACK, P], U8, name="wa_sc", tag="ws_bf11", align_bytes=64)
@@ -177,24 +192,25 @@ def tile_list_expert_under_shared_gate_pl_kernel(
             )
             nc.sync.dma_start(out=out_words[:, cols], in_=y_codes[:, cols].bitcast(I32))
 
+        half = J // 2
         for t in range(PACK):
             drain_u(t)
-            if t < PACK - 1:
+            if t < 2:
                 look_up(t, 0, J)
-        for t in range(PACK - 1):
+        for j0 in (0, half):
+            for t in (2, 3):
+                look_up(t, j0, j0 + half)
+        for t in range(2):
             gated(t, 0, J)
             nc.sync.dma_start(out=out_rows[:, t, :], in_=y[:, t, :])
-        look_up(3, 0, J // 2)
-        look_up(3, J // 2, J)
-        gated(3, 0, J // 2)
-        regroup(nc.vector.tensor_copy, 0, 128)
-        regroup(nc.scalar.copy, 128, 256)
-        gated(3, J // 2, J)
-        nc.sync.dma_start(out=out_rows[:, 3, :], in_=y[:, 3, :])
-        regroup(nc.vector.tensor_copy, 256, 448)
-        regroup(nc.scalar.copy, 448, 512)
-        planes(0)
+        for j0 in (0, half):
+            for t in (2, 3):
+                gated(t, j0, j0 + half)
+            nc.sync.dma_start(out=out_rows[:, 2:4, j0 : j0 + half], in_=y[:, 2:4, j0 : j0 + half])
+        regroup(nc.scalar.copy, 0, half)
+        regroup(nc.vector.tensor_copy, half, J)
         planes(1)
+        planes(0)
         for Q in range(4):
             queue = nc.sync if Q % 2 == 0 else nc.scalar
             queue.dma_start(

@@ -33,7 +33,7 @@ def tile_list_expert_under_shared_gate_pl_kernel(
 
         offsets = keep.tile([P, J // 16], U16, name="offsets")
 
-        row_runs = [[(0, 4)], [(0, 2), (2, 4)]]
+        row_runs = [[(0, 2), (2, 4)], [(0, 2), (2, 4)]]
         ws_raw = [
             [keep.tile([P, j1 - j0, N], F32, name="ws_raw%d%d" % (a, j0), align_bytes=64) for j0, j1 in row_runs[a]]
             for a in range(PASSES)
@@ -55,9 +55,9 @@ def tile_list_expert_under_shared_gate_pl_kernel(
         nc.vector.memset(warm[:], 0.0)
         nc.vector.memset(wa_sc_raw[:].bitcast(U32), 0)
 
-        nc.sync.dma_start(offsets[:], offs)
         for r in range(4):
-            nc.scalar.dma_start(
+            queue = nc.sync if r % 2 == 0 else nc.scalar
+            queue.dma_start(
                 out=xq_sc[r:P:32, :, :].bitcast(I32),
                 in_=xq_scales[:, r:16:4, :].rearrange("z q c -> q z c").bitcast(I32),
             )
@@ -71,6 +71,7 @@ def tile_list_expert_under_shared_gate_pl_kernel(
             if a == 0:
                 nc.sync.dma_start(out=wa_raw[:].bitcast(I32), in_=wa_words[0].bitcast(I32))
         nc.sync.dma_start(out=xq_second[:].bitcast(I32), in_=xq_words[1].bitcast(I32))
+        nc.sync.dma_start(offsets[:], offs)
         nc.scalar.activation(warm_out[:], warm[:], SIGMOID)
         nc.sync.dma_start(
             out=xe_sb[:].bitcast(I32), in_=xe_words[0].rearrange("p c r -> p (c r)").bitcast(I32)
@@ -126,7 +127,7 @@ def tile_list_expert_under_shared_gate_pl_kernel(
         for t in range(PACK):
             cols = slice(P * (t % 2), P * (t % 2 + 1))
             for h in range(HALVES):
-                order = [0, 1] if h == 0 or t == 0 else [1, 0]
+                order = [0, 1] if h == 0 or t < 2 else [1, 0]
                 for a in order:
                     nc.tensor.matmul_mx(
                         out=u_bank[t][h][:],
@@ -154,7 +155,7 @@ def tile_list_expert_under_shared_gate_pl_kernel(
         def drain_u(t):
             for h in range(HALVES):
                 cols = slice(BANK * h, BANK * (h + 1))
-                if h == 0 and t == 0:
+                if h == 0 and t < 2:
                     nc.scalar.copy(out=u_sb[t][:, cols], in_=u_bank[t][h][:])
                 else:
                     nc.vector.tensor_copy(out=u_sb[t][:, cols], in_=u_bank[t][h][:])
@@ -207,10 +208,11 @@ def tile_list_expert_under_shared_gate_pl_kernel(
             for t in (2, 3):
                 gated(t, j0, j0 + half)
             nc.sync.dma_start(out=out_rows[:, 2:4, j0 : j0 + half], in_=y[:, 2:4, j0 : j0 + half])
-        regroup(nc.scalar.copy, 0, half)
+        regroup(nc.scalar.copy, 0, 192)
+        regroup(nc.vector.tensor_copy, 192, half)
         regroup(nc.vector.tensor_copy, half, J)
-        planes(1)
         planes(0)
+        planes(1)
         for Q in range(4):
             queue = nc.sync if Q % 2 == 0 else nc.scalar
             queue.dma_start(

from contextlib import ExitStack

import concourse.mybir as mybir

K, T, J, L, N = 1024, 1024, 512, 512, 512
FLOPS = 2 * K * N * T + 2 * L * N * J

F32 = mybir.dt.float32
BF16 = mybir.dt.bfloat16
I32 = mybir.dt.int32
U32 = mybir.dt.uint32
U16 = mybir.dt.uint16
U8 = mybir.dt.uint8
FP8X4 = mybir.dt.float8_e4m3fn_x4
FP4X4 = mybir.dt.float4_e2m1fn_x4
SIGMOID = mybir.ActivationFunctionType.Sigmoid
MULT = mybir.AluOpType.mult

P = 128
PACK = 4
PASSES = K // (P * PACK)
BANK = 512
HALVES = T // BANK


def tile_list_expert_under_shared_gate_pl_kernel(
    tc, xq_words, xq_scales, ws, xe_words, xe_scales, wa_words, wa_scales, offs, out_0, out_1, out_2
):
    nc = tc.nc
    with ExitStack() as ctx:
        keep = ctx.enter_context(tc.tile_pool(name="keep", bufs=1))
        psum = ctx.enter_context(tc.psum_pool(name="psum", bufs=1))

        offsets = keep.tile([P, J // 16], U16, name="offsets")

        row_runs = [[(0, 2), (2, 4)], [(0, 2), (2, 4)]]
        ws_raw = [
            [keep.tile([P, j1 - j0, N], F32, name="ws_raw%d%d" % (a, j0), align_bytes=64) for j0, j1 in row_runs[a]]
            for a in range(PASSES)
        ]
        xq_first = [keep.tile([P, 2 * BANK], U8, name="xq_first%d" % h, align_bytes=64) for h in range(HALVES)]
        xq_second = keep.tile([P, 2 * T], U8, name="xq_second", align_bytes=64)
        xq_sb = [
            [xq_first[h][:] for h in range(HALVES)],
            [xq_second[:, 2 * BANK * h : 2 * BANK * (h + 1)] for h in range(HALVES)],
        ]
        xq_sc = keep.tile([P, PASSES, T], U8, name="xq_sc", align_bytes=64)
        wa_raw = keep.tile([P, 2 * N], U8, name="wa_raw", align_bytes=64)
        wa_sc_raw = keep.tile([P, N], U8, name="wa_sc_raw", align_bytes=64)
        xe_sb = keep.tile([P, PACK * J], U8, name="xe_sb", align_bytes=64)
        xe_sc = keep.tile([P, J], U8, name="xe_sc", align_bytes=64)

        warm = keep.tile([P, 8], F32, name="warm")
        warm_out = keep.tile([P, 8], F32, name="warm_out")
        nc.vector.memset(warm[:], 0.0)
        nc.vector.memset(wa_sc_raw[:].bitcast(U32), 0)

        for r in range(4):
            queue = nc.sync if r % 2 == 0 else nc.scalar
            queue.dma_start(
                out=xq_sc[r:P:32, :, :].bitcast(I32),
                in_=xq_scales[:, r:16:4, :].rearrange("z q c -> q z c").bitcast(I32),
            )
        for a in range(PASSES):
            rows = ws[512 * a : 512 * (a + 1), :].rearrange("(p j) n -> p j n", j=PACK)
            for raw, (j0, j1) in zip(ws_raw[a], row_runs[a]):
                nc.sync.dma_start(out=raw[:], in_=rows[:, j0:j1, :])
            nc.sync.dma_start(
                out=xq_first[a][:].bitcast(I32), in_=xq_words[0, :, 2 * BANK * a : 2 * BANK * (a + 1)].bitcast(I32)
            )
            if a == 0:
                nc.sync.dma_start(out=wa_raw[:].bitcast(I32), in_=wa_words[0].bitcast(I32))
        nc.sync.dma_start(out=xq_second[:].bitcast(I32), in_=xq_words[1].bitcast(I32))
        nc.sync.dma_start(offsets[:], offs)
        nc.scalar.activation(warm_out[:], warm[:], SIGMOID)
        nc.sync.dma_start(
            out=xe_sb[:].bitcast(I32), in_=xe_words[0].rearrange("p c r -> p (c r)").bitcast(I32)
        )
        for r in range(4):
            nc.sync.dma_start(
                out=wa_sc_raw[r:P:32, :].bitcast(I32),
                in_=wa_scales[0, r:16:4, :].bitcast(I32),
            )
        for r in range(4):
            nc.sync.dma_start(
                out=xe_sc[r:P:32, :].bitcast(I32),
                in_=xe_scales[0, r:16:4, :].bitcast(I32),
            )

        u_bank = [
            [psum.tile([P, BANK], F32, name="u_bank%d%d" % (t, h), tag="bank%d%d" % (t, h)) for h in range(HALVES)]
            for t in range(PACK)
        ]

        ws_codes, ws_scales = [], []
        for a in range(PASSES):
            grouped = [
                keep.tile([P, 2, P, PACK], BF16, name="ws_bf%d%d" % (a, u), tag="ws_bf%d%d" % (a, u), align_bytes=64) for u in range(2)
            ]
            for raw, (j0, j1) in zip(ws_raw[a], row_runs[a]):
                src = raw[:].rearrange("p j (m t) -> p m j t", t=PACK)
                dst = [g[:].rearrange("p t m j -> p m j t")[:, :, j0:j1, :] for g in grouped]
                nc.vector.tensor_copy(out=dst[0], in_=src[:, :, :, 0:2])
                nc.scalar.copy(out=dst[1], in_=src[:, :, :, 2:4])
            codes = [keep.tile([P, 2 * P], U32, name="ws_codes%d%d" % (a, u), align_bytes=64) for u in range(2)]
            scales = [keep.tile([P, 2 * P], U8, name="ws_scales%d%d" % (a, u), align_bytes=64) for u in range(2)]
            for e in range(2):
                nc.vector.quantize_mx(
                    out=codes[0][:, P * e : P * (e + 1)].bitcast(FP8X4),
                    scales=scales[0][:, P * e : P * (e + 1)],
                    in_=grouped[0][:, e, :, :].rearrange("p m j -> p (m j)"),
                )
            nc.vector.quantize_mx(
                out=codes[1][:].bitcast(FP8X4),
                scales=scales[1][:],
                in_=grouped[1][:].rearrange("p t m j -> p (t m j)"),
            )
            ws_codes.append(codes)
            ws_scales.append(scales)
            if a == 0:
                wa_sb = keep.tile([P, PACK, 2 * P], U8, name="wa_sb", tag="ws_bf01", align_bytes=64)
                nc.vector.tensor_copy(
                    out=wa_sb[:].rearrange("p t (m b) -> p t m b", b=2),
                    in_=wa_raw[:].rearrange("p (m t b) -> p t m b", t=PACK, b=2),
                )

        for t in range(PACK):
            cols = slice(P * (t % 2), P * (t % 2 + 1))
            for h in range(HALVES):
                order = [0, 1] if h == 0 or t < 2 else [1, 0]
                for a in order:
                    nc.tensor.matmul_mx(
                        out=u_bank[t][h][:],
                        lhsT=ws_codes[a][t // 2][:, cols].bitcast(FP8X4),
                        lhsT_scale=ws_scales[a][t // 2][:, cols],
                        rhs=xq_sb[a][h].bitcast(FP4X4),
                        rhs_scale=xq_sc[:, a, BANK * h : BANK * (h + 1)],
                        start=(a == order[0]),
                        stop=(a == order[-1]),
                    )

        wa_sc = keep.tile([P, PACK, P], U8, name="wa_sc", tag="ws_bf11", align_bytes=64)
        nc.gpsimd.tensor_copy(out=wa_sc[:], in_=wa_sc_raw[:].rearrange("p (m t) -> p t m", t=PACK))

        u_sb = [keep.tile([P, T], F32, name="u_sb%d" % t, align_bytes=64) for t in range(PACK)]
        gate = [keep.tile([P, J], F32, name="gate%d" % t, align_bytes=64) for t in range(PACK)]
        y = keep.tile([P, PACK, J], F32, name="y", align_bytes=64)
        y_bf = [keep.tile([P, J // 2, PACK], BF16, name="y_bf%d" % g, align_bytes=64) for g in range(2)]
        y_codes = keep.tile([P, J], U32, name="y_codes", align_bytes=64)
        y_scales = keep.tile([P, J], U8, name="y_scales", align_bytes=64)
        out_rows = out_0.rearrange("(p t) j -> p t j", t=PACK)
        out_words = out_1[0].rearrange("p c r -> p (c r)").bitcast(I32)
        p_bank = []

        def drain_u(t):
            for h in range(HALVES):
                cols = slice(BANK * h, BANK * (h + 1))
                if h == 0 and t < 2:
                    nc.scalar.copy(out=u_sb[t][:, cols], in_=u_bank[t][h][:])
                else:
                    nc.vector.tensor_copy(out=u_sb[t][:, cols], in_=u_bank[t][h][:])
            bank = psum.tile([P, BANK], F32, name="p_bank%d" % t, tag="bank%d0" % t)
            nc.tensor.matmul_mx(
                out=bank[:],
                lhsT=wa_sb[:, t, :].bitcast(FP4X4),
                lhsT_scale=wa_sc[:, t, :],
                rhs=xe_sb[:].bitcast(FP8X4),
                rhs_scale=xe_sc[:],
                start=True,
                stop=True,
            )
            p_bank.append(bank)

        def look_up(t, j0, j1):
            nc.scalar.activation(gate[t][:, j0:j1], u_sb[t][:].indirect(offsets[:, j0 // 16 : j1 // 16]), SIGMOID)

        def gated(t, j0, j1):
            nc.vector.tensor_tensor(y[:, t, j0:j1], p_bank[t][:, j0:j1], gate[t][:, j0:j1], MULT)

        def regroup(copy, j0, j1):
            g, first = divmod(j0, J // 2)
            copy(
                out=y_bf[g][:, first : first + j1 - j0, :].rearrange("p (c i) t -> p c t i", i=4),
                in_=y[:, :, j0:j1].rearrange("p t (c i) -> p c t i", i=4),
            )

        def planes(g):
            cols = slice(g * J // 2, (g + 1) * J // 2)
            nc.vector.quantize_mx(
                out=y_codes[:, cols].bitcast(FP8X4),
                scales=y_scales[:, cols],
                in_=y_bf[g][:].rearrange("p c t -> p (c t)"),
            )
            nc.sync.dma_start(out=out_words[:, cols], in_=y_codes[:, cols].bitcast(I32))

        half = J // 2
        for t in range(PACK):
            drain_u(t)
            if t < 2:
                look_up(t, 0, J)
        for j0 in (0, half):
            for t in (2, 3):
                look_up(t, j0, j0 + half)
        for t in range(2):
            gated(t, 0, J)
            nc.sync.dma_start(out=out_rows[:, t, :], in_=y[:, t, :])
        for j0 in (0, half):
            for t in (2, 3):
                gated(t, j0, j0 + half)
            nc.sync.dma_start(out=out_rows[:, 2:4, j0 : j0 + half], in_=y[:, 2:4, j0 : j0 + half])
        regroup(nc.scalar.copy, 0, 192)
        regroup(nc.vector.tensor_copy, 192, half)
        regroup(nc.vector.tensor_copy, half, J)
        planes(0)
        planes(1)
        for Q in range(4):
            queue = nc.sync if Q % 2 == 0 else nc.scalar
            queue.dma_start(
                out=out_2[0, 4 * Q : 4 * Q + 4, :].bitcast(I32),
                in_=y_scales[32 * Q : 32 * Q + 4, :].bitcast(I32),
            )
